import numpy as np
import ml_dtypes


def mxq(x, axis, fmt="e4m3"):
    dtype, down = {"e4m3": (ml_dtypes.float8_e4m3fn, 7), "e5m2": (ml_dtypes.float8_e5m2, 14)}[fmt]
    v = np.moveaxis(np.asarray(x, np.float32).astype(ml_dtypes.bfloat16).astype(np.float64), axis, -1)
    blocks = v.reshape(v.shape[:-1] + (-1, 32))
    amax = np.abs(blocks).max(-1, keepdims=True)
    byte = np.maximum(np.where(amax > 0, np.frexp(amax)[1] - 1 + 127, 0) - down, 1)
    scale = np.exp2(byte - 127.0)
    codes = (blocks / scale).astype(np.float32).astype(dtype).astype(np.float64)
    return np.moveaxis((codes * scale).reshape(v.shape), -1, axis)


WIDE = False


def mx_kscale(k):
    if not WIDE:
        return np.ones(k)
    levels = np.array([10, -10, 5, -5, 0])
    if k % 512:
        return np.exp2(np.random.permutation(np.resize(levels, k // 32))).repeat(32)
    a = np.empty((k // 512, 16))
    for p in range(k // 512):
        a[p, :8] = np.random.permutation(np.resize(levels, 8))
        for g in range(8):
            far = levels[np.abs(levels - a[p, g]) >= 10]
            a[p, g + 8] = far[np.random.randint(len(far))]
    return np.exp2(a.ravel()).repeat(32)


def f64(x):
    return np.asarray(x).astype(np.float64)


def striped(idx):
    return np.tile(idx.reshape(-1, 16).T, (8, 1)).astype(np.uint16)


def unstriped(offs):
    return offs[:16].T.reshape(-1).astype(np.int64)


def striped8(idx):
    return np.concatenate([x.reshape(-1, 16).T for x in idx]).astype(np.uint16)


def runs(offs, k):
    lists = np.stack([offs[16 * r : 16 * r + 16].T.reshape(-1) for r in range(8)]).astype(np.int64)
    return lists[np.arange(k) % 512 // 64]


def pack_weight(w):
    k, n = w.shape
    w = f64(np.asarray(w, np.float32).astype(ml_dtypes.bfloat16)).reshape(k // 32, 32, n)
    amax = np.abs(w).max(1)
    byte = np.clip(np.where(amax > 0, np.frexp(amax)[1] - 1 + 127 - 7, 1), 1, 254)
    scaled = (w * np.exp2(127.0 - byte)[:, None, :]).reshape(k, n).astype(np.float32)
    words = np.ascontiguousarray(scaled.reshape(k // 512, 128, 4, n).transpose(0, 1, 3, 2)).astype(ml_dtypes.float8_e4m3fn).view(np.uint8)
    return words, np.ascontiguousarray(byte.astype(np.uint8).reshape(k // 512, 16, n))


def unpack_weight(words, scales):
    g, p, n, _ = words.shape
    vals = np.ascontiguousarray(words).view(ml_dtypes.float8_e4m3fn).astype(np.float64) * np.repeat(np.exp2(scales.astype(np.float64) - 127.0), 8, axis=1)[..., None]
    return vals.transpose(0, 1, 3, 2).reshape(g * 512, n)


E2M1 = np.array([0.0, 0.5, 1.0, 1.5, 2.0, 3.0, 4.0, 6.0, -0.0, -0.5, -1.0, -1.5, -2.0, -3.0, -4.0, -6.0])


def pack_fp4(w):
    k, n = w.shape
    w = f64(np.asarray(w, np.float32).astype(ml_dtypes.bfloat16)).reshape(k // 32, 32, n)
    amax = np.abs(w).max(1)
    mant, ex = np.frexp(amax / 6.0)
    byte = np.clip(np.where(amax > 0, np.where(mant > 0.5, ex, ex - 1) + 127, 1), 1, 254)
    scaled = (w * np.exp2(127.0 - byte)[:, None, :]).reshape(k, n).astype(np.float32)
    c = np.ascontiguousarray(scaled.reshape(k // 512, 128, 4, n).transpose(0, 1, 3, 2)).astype(ml_dtypes.float4_e2m1fn).view(np.uint8) & 0xF
    words = (c[..., 0::2] | (c[..., 1::2] << 4)).reshape(k // 512, 128, 2 * n)
    return np.ascontiguousarray(words), np.ascontiguousarray(byte.astype(np.uint8).reshape(k // 512, 16, n))


def unpack_fp4(words, scales):
    g, _, n = scales.shape
    words = np.ascontiguousarray(words).reshape(g, 128, n, 2)
    nib = np.empty((g, 128, n, 4), np.uint8)
    nib[..., 0::2] = words & 0xF
    nib[..., 1::2] = words >> 4
    vals = E2M1[nib] * np.repeat(np.exp2(scales.astype(np.float64) - 127.0), 8, axis=1)[..., None]
    return vals.transpose(0, 1, 3, 2).reshape(g * 512, n)


def planes(y):
    n, m = y.shape
    v = y.astype(np.float32).astype(ml_dtypes.bfloat16).astype(np.float64).reshape(n // 32, 32, m)
    top = np.abs(v).max(1)
    byte = np.clip(np.where(top > 0, np.frexp(top)[1] - 1 + 127 - 7, 1), 1, 254)
    codes = (v * np.exp2(127.0 - byte)[:, None, :]).reshape(n, m).astype(np.float32).astype(ml_dtypes.float8_e4m3fn).view(np.uint8)
    words = codes.reshape(n // 512, 128, 4, m).transpose(0, 1, 3, 2)
    return np.ascontiguousarray(words), np.ascontiguousarray(byte.astype(np.uint8).reshape(n // 512, 16, m))


K, T, S, H, C = 512, 2048, 512, 512, 512


def setup_inputs():
    n = np.random.standard_normal
    s = mx_kscale(K)[:, None]
    packed_xT = pack_weight(n((K, T)) * s)
    packed_w1 = pack_fp4(n((K, H)) / np.sqrt(K) / s)
    return {
        "x_words": packed_xT[0],
        "x_scales": packed_xT[1],
        "w1_words": packed_w1[0],
        "w1_scales": packed_w1[1],
        "tau": np.random.uniform(0.3, 0.9, (H, 1)).astype(np.float32),
        "gs": (np.random.uniform(0.5, 1.5, (K, 1)) / s).astype(np.float32),
        "tau2": np.random.uniform(0.3, 0.9, (C, 1)).astype(np.float32),
        "offs": striped(np.random.permutation(T)[:S]),
        "n1": striped(np.random.permutation(S)),
        "n2": striped(np.random.permutation(S)),
        "ca": striped(np.random.permutation(T)[:C]),
        "hc": striped8(np.random.randint(0, T, (8, C))),
        "n3": striped8(np.stack([np.random.permutation(S) for _ in range(8)])),
        "n4": striped8(np.stack([np.random.permutation(S) for _ in range(8)])),
    }


def reference(x_words, x_scales, w1_words, w1_scales, tau, gs, tau2, offs, n1, n2, ca, hc, n3, n4):
    x_hc = unpack_weight(x_words, x_scales)[np.arange(K)[:, None], runs(hc, K)]
    xq = unpack_weight(x_words, x_scales)[:, unstriped(offs)]
    y = unpack_fp4(w1_words, w1_scales).T @ xq
    top = y.max(axis=1, keepdims=True)
    ea = np.exp(f64(tau) * (y[:, unstriped(n1)] - top))
    sm = y * ea
    ds = np.zeros((H, S))
    ds[:, unstriped(n2)] = sm
    z = f64(gs) * (2.0 * ds - (0.5 * y))
    zq = mxq(z, 0, "e4m3")
    b = 0.0625 * (x_hc.T @ zq)
    top2 = b.max(axis=1, keepdims=True)
    ea2 = np.exp(f64(tau2) * (b[np.arange(C)[:, None], runs(n3, C)] - top2))
    x_ca = unpack_weight(x_words, x_scales)[:, unstriped(ca)]
    a = 0.0625 * (x_ca.T @ zq)
    out_0 = (2.0 * ea2) * (a - (a[np.arange(C)[:, None], runs(n4, C)])) - (0.5 * b)
    return (out_0,) + planes(out_0)

@@ -1,0 +1,292 @@
+from contextlib import ExitStack
+
+import concourse.mybir as mybir
+
+K, T, S = 512, 2048, 512
+P = 128
+PACK = 4
+HALF = S // 2
+LIST_COLS = S // 16
+FLOPS = 3 * 2 * K * S * S
+
+F32 = mybir.dt.float32
+BF16 = mybir.dt.bfloat16
+I32 = mybir.dt.int32
+U32 = mybir.dt.uint32
+U16 = mybir.dt.uint16
+U8 = mybir.dt.uint8
+FP8X4 = mybir.dt.float8_e4m3fn_x4
+FP4X4 = mybir.dt.float4_e2m1fn_x4
+MULT = mybir.AluOpType.mult
+ADD = mybir.AluOpType.add
+SUB = mybir.AluOpType.subtract
+MAX = mybir.AluOpType.max
+EXP = mybir.ActivationFunctionType.Exp
+COPY = mybir.ActivationFunctionType.Copy
+
+OUT_CHUNKS = ((0, 256), (256, 256))
+A_ON_VECTOR = ()
+PROD_G = ()
+IL_S = ()
+OTHER_V = ()
+
+
+def entries(lst, first, count):
+    return lst[:, first // 16 : (first + count) // 16]
+
+
+def tile_picked_cdhpxbesd_none_po_kernel(
+    tc, x_words, x_scales, w1_words, w1_scales, tau, gs, tau2, offs, n1, n2, ca, hc, n3, n4, out_0, out_1, out_2
+):
+    nc = tc.nc
+    with ExitStack() as ctx:
+        keep = ctx.enter_context(tc.tile_pool(name="keep", bufs=1))
+        psum = ctx.enter_context(tc.psum_pool(name="psum", bufs=1))
+
+        def sb(name, shape, dtype, tag=None):
+            return keep.tile(shape, dtype, name=name, tag=tag or name, align_bytes=64)
+
+        def load_list(name, src):
+            lst = sb(name, [P, LIST_COLS], U16)
+            nc.sync.dma_start(lst[:], src)
+            return lst
+
+        def load_rows(name, src):
+            col = sb(name, [P, PACK], F32)
+            nc.sync.dma_start(col[:], src.rearrange("(p t) o -> p (t o)", t=PACK))
+            return col
+
+        def load_plane(plane, src, quadrants):
+            for q in quadrants:
+                rows = src[0, 4 * q : 4 * q + 4, :].bitcast(I32)
+                nc.sync.dma_start(plane[32 * q : 32 * q + 32, :].bitcast(I32), rows.partition_broadcast(8))
+
+        xs = sb("xs", [P, T], U8)
+        load_plane(xs, x_scales, range(4))
+        offs_l = load_list("offs_l", offs)
+        w1w_raw = sb("w1w_raw", [P, 2 * S], U8)
+        nc.sync.dma_start(w1w_raw[:].bitcast(I32), w1_words[0].bitcast(I32))
+        w1s_raw = sb("w1s_raw", [P, S], U8)
+        load_plane(w1s_raw, w1_scales, range(1))
+        xw = sb("xw", [P, T], U32)
+        nc.sync.dma_start(xw[:].bitcast(I32), x_words[0].rearrange("p n t -> p (n t)").bitcast(I32))
+        load_plane(w1s_raw, w1_scales, range(1, 4))
+        tau_c = load_rows("tau_c", tau)
+        n1_l = load_list("n1_l", n1)
+        gs_c = load_rows("gs_c", gs)
+        n2_l = load_list("n2_l", n2)
+        ca_l = load_list("ca_l", ca)
+        hc_l = load_list("hc_l", hc)
+        tau2_c = load_rows("tau2_c", tau2)
+        n3_l = load_list("n3_l", n3)
+        n4_l = load_list("n4_l", n4)
+
+        xq_s = sb("xq_s", [P, S], U8)
+        nc.vector.tensor_copy(xq_s[:], xs[:].indirect(offs_l[:]))
+        w1w = sb("w1w", [P, 2 * S], U8)
+        nc.scalar.copy(
+            w1w[:].bitcast(U16).rearrange("p (t m) -> p t m", t=PACK),
+            w1w_raw[:].bitcast(U16).rearrange("p (m t) -> p t m", t=PACK),
+        )
+        w1s = sb("w1s", [P, PACK, P], U8)
+        w1s_dealt = w1s_raw[:].rearrange("p (m t) -> p t m", t=PACK)
+        xq_w = sb("xq_w", [P, S], U32)
+        nc.vector.tensor_copy(xq_w[:], xw[:].indirect(offs_l[:]))
+        for planes in (slice(0, 1), slice(1, PACK)):
+            nc.vector.tensor_copy(w1s[:, planes, :], w1s_dealt[:, planes, :])
+        neg_tau = sb("neg_tau", [P, PACK], F32)
+        nc.gpsimd.tensor_scalar(neg_tau[:], tau_c[:], -1.0, 0.0, MULT, ADD)
+        neg_tau2 = sb("neg_tau2", [P, PACK], F32)
+        nc.gpsimd.tensor_scalar(neg_tau2[:], tau2_c[:], -1.0, 0.0, MULT, ADD)
+        gs_sm = sb("gs_sm", [P, PACK], F32)
+        nc.gpsimd.tensor_scalar(gs_sm[:], gs_c[:], 2.0, 0.0, MULT, ADD)
+        gs_y = sb("gs_y", [P, PACK], F32)
+        nc.gpsimd.tensor_scalar(gs_y[:], gs_c[:], -0.5, 0.0, MULT, ADD)
+
+        def product(acc, lhs_w, lhs_s, rhs_w, rhs_s, pieces):
+            width = S // pieces
+            for i in range(pieces):
+                cols = slice(i * width, (i + 1) * width)
+                nc.tensor.matmul_mx(
+                    out=acc[:, cols],
+                    lhsT=lhs_w,
+                    lhsT_scale=lhs_s,
+                    rhs=rhs_w[:, cols].bitcast(FP8X4),
+                    rhs_scale=rhs_s[:, cols],
+                    start=True,
+                    stop=True,
+                )
+
+        def leave_bank_with_bias(name, acc, factor, rate, on_scalar=False):
+            rows = sb(name, [P, S], F32)
+            top = sb(name + "_top", [P, 1], F32)
+            nc.vector.tensor_scalar(rows[:], acc[:], factor, None, MULT, MAX, accum_out=top[:])
+            bias = sb(name + "_bias", [P, 1], F32)
+            if on_scalar:
+                nc.scalar.activation(bias[:], top[:], COPY, scale=rate)
+            else:
+                nc.gpsimd.tensor_scalar(bias[:], top[:], rate, 0.0, MULT, ADD)
+            return rows, bias
+
+        y, y_bias = [], []
+        for t in range(PACK):
+            acc = psum.tile([P, S], F32, name="bank%d" % t)
+            product(
+                acc,
+                w1w[:, 2 * P * t : 2 * P * (t + 1)].bitcast(FP4X4),
+                w1s[:, t, :],
+                xq_w,
+                xq_s,
+                1,
+            )
+            rows, bias = leave_bank_with_bias("y%d" % t, acc, 1.0, neg_tau[:, t : t + 1], t == 0)
+            y.append(rows)
+            y_bias.append(bias)
+
+        sm = [sb("sm%d" % t, [P, S], F32) for t in range(PACK)]
+        ds = [sb("ds%d" % t, [P, S], F32) for t in range(PACK)]
+        ea = [sb("ea%d" % t, [P, S], F32) for t in range(PACK)]
+
+        def fetch_ea(t, h):
+            cols = slice(h * HALF, (h + 1) * HALF)
+            nc.scalar.activation(
+                ea[t][:, cols],
+                y[t][:].indirect(entries(n1_l, h * HALF, HALF)),
+                EXP,
+                bias=y_bias[t][:],
+                scale=tau_c[:, t : t + 1],
+            )
+
+        def make_sm(t, h):
+            cols = slice(h * HALF, (h + 1) * HALF)
+            nc.vector.scalar_tensor_tensor(sm[t][:, cols], y[t][:, cols], gs_sm[:, t : t + 1], ea[t][:, cols], MULT, MULT)
+
+        def put_sm(t, h):
+            cols = slice(h * HALF, (h + 1) * HALF)
+            nc.scalar.activation(ds[t][:].indirect(entries(n2_l, h * HALF, HALF)), sm[t][:, cols], COPY)
+
+        z_in = [sb("z_in%d" % h, [P, HALF, PACK], BF16) for h in range(2)]
+        z_w = sb("z_w", [P, S], U32)
+        z_s = sb("z_s", [P, S], U8)
+
+        def make_z(t):
+            halves = []
+            for h in range(2):
+                cols = slice(h * HALF, (h + 1) * HALF)
+                z_half = sb("z_half%d" % h, [P, HALF], BF16)
+                nc.vector.scalar_tensor_tensor(z_half[:], y[t][:, cols], gs_y[:, t : t + 1], ds[t][:, cols], MULT, ADD)
+                halves.append(z_half)
+            for h in range(2):
+                nc.vector.tensor_copy(z_in[h][:, :, t], halves[h][:])
+
+        hc_w = sb("hc_w", [P, S], U32)
+        hc_s_dealt = sb("hc_s_dealt", [P, S], U8)
+        hc_s = sb("hc_s", [P, S], U8)
+        nc.gpsimd.memset(hc_s[:].bitcast(I32), 0)
+        picked = {}
+
+        def pick_hc_scales():
+            hc_s_raw = sb("hc_s_raw", [P, S], U8, "ea0")
+            nc.vector.tensor_copy(hc_s_raw[:], xs[:].indirect(hc_l[:]))
+            nc.vector.tensor_copy(
+                hc_s_dealt[:].rearrange("p (t m) -> p t m", t=PACK), hc_s_raw[:].rearrange("p (m t) -> p t m", t=PACK)
+            )
+            for r in range(4):
+                src = r + 16 * (r // 2)
+                nc.sync.dma_start(hc_s[r:P:32, :].bitcast(I32), hc_s_dealt[src:P:32, :].bitcast(I32))
+
+        def pick_hc_words():
+            hc_w_raw = sb("hc_w_raw", [P, S], U32, "ea1")
+            nc.vector.tensor_copy(hc_w_raw[:], xw[:].indirect(hc_l[:]))
+            nc.vector.tensor_copy(
+                hc_w[:].rearrange("p (t m) -> p t m", t=PACK), hc_w_raw[:].rearrange("p (m t) -> p t m", t=PACK)
+            )
+
+        def pick_ca_words():
+            picked["ca_w"] = sb("ca_w", [P, S], U32, "ea2")
+            nc.vector.tensor_copy(picked["ca_w"][:].rearrange("p (t m) -> p m t", t=PACK), xw[:].indirect(ca_l[:]))
+
+        def pick_ca_scales():
+            picked["ca_s"] = sb("ca_s", [P, S], U8, "ea3")
+            nc.vector.tensor_copy(picked["ca_s"][:].rearrange("p (t m) -> p m t", t=PACK), xs[:].indirect(ca_l[:]))
+
+        picks = [pick_hc_scales, pick_hc_words, pick_ca_words, pick_ca_scales]
+
+        for t in range(PACK):
+            for h in range(2):
+                fetch_ea(t, h)
+        for pair in range(0, PACK, 2):
+            for h in range(2):
+                for t in (pair, pair + 1):
+                    make_sm(t, h)
+                    put_sm(t, h)
+        for pick in picks:
+            pick()
+        for t in range(PACK):
+            make_z(t)
+        ca_w, ca_s = picked["ca_w"], picked["ca_s"]
+        for h in range(2):
+            cols = slice(h * HALF, (h + 1) * HALF)
+            nc.vector.quantize_mx(
+                out=z_w[:, cols].bitcast(FP8X4), scales=z_s[:, cols], in_=z_in[h][:].rearrange("p c t -> p (c t)")
+            )
+
+        a2, b, b_bias, accs = [], [], [], []
+        for t in range(PACK):
+            m_cols = slice(P * t, P * (t + 1))
+            acc_a = psum.tile([P, S], F32, name="bank%d" % ((4 + 2 * t) % 8))
+            product(acc_a, ca_w[:, m_cols].bitcast(FP8X4), ca_s[:, m_cols], z_w, z_s, 1)
+            acc_b = psum.tile([P, S], F32, name="bank%d" % ((5 + 2 * t) % 8))
+            product(acc_b, hc_w[:, m_cols].bitcast(FP8X4), hc_s[:, m_cols], z_w, z_s, 1)
+            rows_a = sb("a2_%d" % t, [P, S], F32)
+            if t in A_ON_VECTOR:
+                nc.vector.tensor_scalar(rows_a[:], acc_a[:], 0.125, None, MULT)
+            else:
+                nc.scalar.activation(rows_a[:], acc_a[:], COPY, scale=0.125)
+            a2.append(rows_a)
+            accs.append((acc_a, acc_b))
+            rows, bias = leave_bank_with_bias("b%d" % t, acc_b, 0.0625, neg_tau2[:, t : t + 1])
+            b.append(rows)
+            b_bias.append(bias)
+
+        out_rows = out_0.rearrange("(p t) j -> p t j", t=PACK)
+        o_w = sb("o_w", [P, S], U32)
+        o_s = sb("o_s", [P, S], U8)
+        for first, width in OUT_CHUNKS:
+            cols = slice(first, first + width)
+            res = sb("res%d" % first, [P, PACK, width], F32)
+            for t in range(PACK):
+                tag = "%d_%d" % (t, first)
+                other = sb("other" + tag, [P, width], F32)
+                if (t, first) in OTHER_V:
+                    nc.vector.tensor_copy(other[:], a2[t][:].indirect(entries(n4_l, first, width)))
+                else:
+                    nc.scalar.activation(other[:], a2[t][:].indirect(entries(n4_l, first, width)), COPY)
+                ea2 = sb("ea2" + tag, [P, width], F32)
+                nc.scalar.activation(
+                    ea2[:],
+                    b[t][:].indirect(entries(n3_l, first, width)),
+                    EXP,
+                    bias=b_bias[t][:],
+                    scale=tau2_c[:, t : t + 1],
+                )
+                diff = sb("diff" + tag, [P, width], F32)
+                nc.vector.scalar_tensor_tensor(diff[:], accs[t][0][:, cols], 0.125, other[:], MULT, SUB)
+                prod = sb("prod" + tag, [P, width], F32)
+                (nc.gpsimd if (t, first) in PROD_G else nc.vector).tensor_tensor(prod[:], diff[:], ea2[:], MULT)
+                nc.vector.scalar_tensor_tensor(res[:, t, :], accs[t][1][:, cols], -0.03125, prod[:], MULT, ADD)
+                nc.sync.dma_start(out_rows[:, t, cols], res[:, t, :])
+            res_in = sb("res_in%d" % first, [P, width, PACK], BF16)
+            if first in IL_S:
+                nc.scalar.copy(res_in[:], res[:].rearrange("p t c -> p c t"))
+            else:
+                nc.vector.tensor_copy(res_in[:], res[:].rearrange("p t c -> p c t"))
+            nc.vector.quantize_mx(
+                out=o_w[:, cols].bitcast(FP8X4), scales=o_s[:, cols], in_=res_in[:].rearrange("p c t -> p (c t)")
+            )
+            nc.sync.dma_start(
+                out_1[0].rearrange("p n t -> p (n t)").bitcast(I32)[:, cols], o_w[:, cols].bitcast(I32)
+            )
+        for q in range(4):
+            queue = nc.scalar if q % 2 == 0 else nc.sync
+            queue.dma_start(out_2[0, 4 * q : 4 * q + 4, :].bitcast(I32), o_s[32 * q : 32 * q + 4, :].bitcast(I32))

@@ -24,11 +24,13 @@ MAX = mybir.AluOpType.max
 EXP = mybir.ActivationFunctionType.Exp
 COPY = mybir.ActivationFunctionType.Copy
 
-OUT_CHUNKS = ((0, 256), (256, 256))
-A_ON_VECTOR = ()
+A_ON_VECTOR = (1, 2, 3)
 PROD_G = ()
-IL_S = ()
-OTHER_V = ()
+SPLIT = (0, 1, 2, 3)
+AHEAD = 4
+IL_S = ((0, 0), (0, 1))
+FUSED = ()
+RING = 99
 
 
 def entries(lst, first, count):
@@ -64,13 +66,13 @@ def tile_picked_cdhpxbesd_none_po_kernel(
         xs = sb("xs", [P, T], U8)
         load_plane(xs, x_scales, range(4))
         offs_l = load_list("offs_l", offs)
-        w1w_raw = sb("w1w_raw", [P, 2 * S], U8)
-        nc.sync.dma_start(w1w_raw[:].bitcast(I32), w1_words[0].bitcast(I32))
         w1s_raw = sb("w1s_raw", [P, S], U8)
-        load_plane(w1s_raw, w1_scales, range(1))
+        load_plane(w1s_raw, w1_scales, range(2))
         xw = sb("xw", [P, T], U32)
         nc.sync.dma_start(xw[:].bitcast(I32), x_words[0].rearrange("p n t -> p (n t)").bitcast(I32))
-        load_plane(w1s_raw, w1_scales, range(1, 4))
+        load_plane(w1s_raw, w1_scales, range(2, 4))
+        w1w_raw = sb("w1w_raw", [P, 2 * S], U8)
+        nc.sync.dma_start(w1w_raw[:].bitcast(I32), w1_words[0].bitcast(I32))
         tau_c = load_rows("tau_c", tau)
         n1_l = load_list("n1_l", n1)
         gs_c = load_rows("gs_c", gs)
@@ -83,19 +85,17 @@ def tile_picked_cdhpxbesd_none_po_kernel(
 
         xq_s = sb("xq_s", [P, S], U8)
         nc.vector.tensor_copy(xq_s[:], xs[:].indirect(offs_l[:]))
-        w1w = sb("w1w", [P, 2 * S], U8)
-        nc.scalar.copy(
-            w1w[:].bitcast(U16).rearrange("p (t m) -> p t m", t=PACK),
-            w1w_raw[:].bitcast(U16).rearrange("p (m t) -> p t m", t=PACK),
-        )
+        w1w = sb("w1w", [P, PACK, P], U16)
+        w1w_dealt = w1w_raw[:].bitcast(U16).rearrange("p (m t) -> p t m", t=PACK)
         w1s = sb("w1s", [P, PACK, P], U8)
         w1s_dealt = w1s_raw[:].rearrange("p (m t) -> p t m", t=PACK)
         xq_w = sb("xq_w", [P, S], U32)
-        nc.vector.tensor_copy(xq_w[:], xw[:].indirect(offs_l[:]))
-        for planes in (slice(0, 1), slice(1, PACK)):
-            nc.vector.tensor_copy(w1s[:, planes, :], w1s_dealt[:, planes, :])
+        for h, planes in enumerate((slice(0, 1), slice(1, PACK))):
+            nc.scalar.copy(w1w[:, planes, :], w1w_dealt[:, planes, :])
+            nc.vector.tensor_copy(xq_w[:, h * HALF : (h + 1) * HALF], xw[:].indirect(entries(offs_l, h * HALF, HALF)))
+            nc.gpsimd.tensor_copy(w1s[:, planes, :], w1s_dealt[:, planes, :])
         neg_tau = sb("neg_tau", [P, PACK], F32)
-        nc.gpsimd.tensor_scalar(neg_tau[:], tau_c[:], -1.0, 0.0, MULT, ADD)
+        nc.vector.tensor_scalar(neg_tau[:], tau_c[:], -1.0, None, MULT)
         neg_tau2 = sb("neg_tau2", [P, PACK], F32)
         nc.gpsimd.tensor_scalar(neg_tau2[:], tau2_c[:], -1.0, 0.0, MULT, ADD)
         gs_sm = sb("gs_sm", [P, PACK], F32)
@@ -103,43 +103,45 @@ def tile_picked_cdhpxbesd_none_po_kernel(
         gs_y = sb("gs_y", [P, PACK], F32)
         nc.gpsimd.tensor_scalar(gs_y[:], gs_c[:], -0.5, 0.0, MULT, ADD)
 
-        def product(acc, lhs_w, lhs_s, rhs_w, rhs_s, pieces):
-            width = S // pieces
-            for i in range(pieces):
-                cols = slice(i * width, (i + 1) * width)
-                nc.tensor.matmul_mx(
-                    out=acc[:, cols],
-                    lhsT=lhs_w,
-                    lhsT_scale=lhs_s,
-                    rhs=rhs_w[:, cols].bitcast(FP8X4),
-                    rhs_scale=rhs_s[:, cols],
-                    start=True,
-                    stop=True,
-                )
+        def product(bank, lhs_w, lhs_s, rhs_w, rhs_s, cols):
+            acc = psum.tile([P, cols.stop - cols.start], F32, name="bank%d" % bank)
+            nc.tensor.matmul_mx(
+                out=acc[:],
+                lhsT=lhs_w,
+                lhsT_scale=lhs_s,
+                rhs=rhs_w[:, cols].bitcast(FP8X4),
+                rhs_scale=rhs_s[:, cols],
+                start=True,
+                stop=True,
+            )
+            return acc
 
-        def leave_bank_with_bias(name, acc, factor, rate, on_scalar=False):
+        def leave_banks_with_bias(name, accs, factor, rate, on_scalar=False):
             rows = sb(name, [P, S], F32)
-            top = sb(name + "_top", [P, 1], F32)
-            nc.vector.tensor_scalar(rows[:], acc[:], factor, None, MULT, MAX, accum_out=top[:])
+            width = S // len(accs)
+            top = None
+            for i, acc in enumerate(accs):
+                so_far = top
+                top = sb("%s_top%d" % (name, i), [P, 1], F32)[:]
+                nc.vector.tensor_scalar(
+                    rows[:, i * width : (i + 1) * width], acc[:], factor, so_far, MULT, MAX, accum_out=top
+                )
             bias = sb(name + "_bias", [P, 1], F32)
             if on_scalar:
-                nc.scalar.activation(bias[:], top[:], COPY, scale=rate)
+                nc.scalar.activation(bias[:], top, COPY, scale=rate)
             else:
-                nc.gpsimd.tensor_scalar(bias[:], top[:], rate, 0.0, MULT, ADD)
+                nc.gpsimd.tensor_scalar(bias[:], top, rate, 0.0, MULT, ADD)
             return rows, bias
 
+        halves = [slice(0, HALF), slice(HALF, S)]
+        whole = [slice(0, S)]
         y, y_bias = [], []
         for t in range(PACK):
-            acc = psum.tile([P, S], F32, name="bank%d" % t)
-            product(
-                acc,
-                w1w[:, 2 * P * t : 2 * P * (t + 1)].bitcast(FP4X4),
-                w1s[:, t, :],
-                xq_w,
-                xq_s,
-                1,
-            )
-            rows, bias = leave_bank_with_bias("y%d" % t, acc, 1.0, neg_tau[:, t : t + 1], t == 0)
+            accs = [
+                product(t + 4 * i, w1w[:, t, :].bitcast(FP4X4), w1s[:, t, :], xq_w, xq_s, cols)
+                for i, cols in enumerate(halves if t == 0 else whole)
+            ]
+            rows, bias = leave_banks_with_bias("y%d" % t, accs, 1.0, neg_tau[:, t : t + 1], t == 0)
             y.append(rows)
             y_bias.append(bias)
 
@@ -231,62 +233,86 @@ def tile_picked_cdhpxbesd_none_po_kernel(
                 out=z_w[:, cols].bitcast(FP8X4), scales=z_s[:, cols], in_=z_in[h][:].rearrange("p c t -> p (c t)")
             )
 
-        a2, b, b_bias, accs = [], [], [], []
-        for t in range(PACK):
-            m_cols = slice(P * t, P * (t + 1))
-            acc_a = psum.tile([P, S], F32, name="bank%d" % ((4 + 2 * t) % 8))
-            product(acc_a, ca_w[:, m_cols].bitcast(FP8X4), ca_s[:, m_cols], z_w, z_s, 1)
-            acc_b = psum.tile([P, S], F32, name="bank%d" % ((5 + 2 * t) % 8))
-            product(acc_b, hc_w[:, m_cols].bitcast(FP8X4), hc_s[:, m_cols], z_w, z_s, 1)
-            rows_a = sb("a2_%d" % t, [P, S], F32)
-            if t in A_ON_VECTOR:
-                nc.vector.tensor_scalar(rows_a[:], acc_a[:], 0.125, None, MULT)
-            else:
-                nc.scalar.activation(rows_a[:], acc_a[:], COPY, scale=0.125)
-            a2.append(rows_a)
-            accs.append((acc_a, acc_b))
-            rows, bias = leave_bank_with_bias("b%d" % t, acc_b, 0.0625, neg_tau2[:, t : t + 1])
-            b.append(rows)
-            b_bias.append(bias)
-
         out_rows = out_0.rearrange("(p t) j -> p t j", t=PACK)
         o_w = sb("o_w", [P, S], U32)
         o_s = sb("o_s", [P, S], U8)
-        for first, width in OUT_CHUNKS:
-            cols = slice(first, first + width)
-            res = sb("res%d" % first, [P, PACK, width], F32)
-            for t in range(PACK):
-                tag = "%d_%d" % (t, first)
-                other = sb("other" + tag, [P, width], F32)
-                if (t, first) in OTHER_V:
-                    nc.vector.tensor_copy(other[:], a2[t][:].indirect(entries(n4_l, first, width)))
-                else:
-                    nc.scalar.activation(other[:], a2[t][:].indirect(entries(n4_l, first, width)), COPY)
-                ea2 = sb("ea2" + tag, [P, width], F32)
+        res = sb("res", [P, PACK, S], F32)
+        res_in = [sb("res_in%d" % h, [P, HALF, PACK], BF16) for h in range(2)]
+        twins, banks, a2, b, b_bias, units = [], [], [], [], [], []
+
+        def open_rows(t):
+            m_cols = slice(P * t, P * (t + 1))
+            accs_a, accs_b = [], []
+            for cols in halves if t == 0 else whole:
+                for accs_x, words, scales in ((accs_a, ca_w, ca_s), (accs_b, hc_w, hc_s)):
+                    bank = (5 + len(banks)) % 8
+                    banks.append(bank)
+                    accs_x.append(product(bank, words[:, m_cols].bitcast(FP8X4), scales[:, m_cols], z_w, z_s, cols))
+            rows_a = sb("a2_%d" % t, [P, S], F32)
+            if t not in A_ON_VECTOR:
+                for acc, cols in zip(accs_a, halves if t == 0 else whole):
+                    nc.scalar.activation(rows_a[:, cols], acc[:], COPY, scale=0.125)
+            rows, bias = leave_banks_with_bias("b%d" % t, accs_b, 0.0625, neg_tau2[:, t : t + 1])
+            if t in A_ON_VECTOR:
+                nc.vector.tensor_scalar(rows_a[:], accs_a[0][:], 0.125, None, MULT)
+            a2.append(rows_a)
+            twin = None
+            if any(tt == t for tt, hh in FUSED):
+                twin = sb("a2_twin%d" % t, [P, S], F32)
+                nc.sync.dma_start(twin[:], rows_a[:])
+            twins.append(twin)
+            b.append(rows)
+            b_bias.append(bias)
+
+        def interleave(h, planes):
+            copy = nc.scalar.copy if (planes.start, h) in IL_S else nc.vector.tensor_copy
+            copy(res_in[h][:, :, planes], res[:, planes, halves[h]].rearrange("p t c -> p c t"))
+
+        def close_rows(t):
+            if (t, 0) not in FUSED or (t, 1) not in FUSED:
+                other = sb("other%d" % t, [P, S], F32)
+            ea2 = sb("ea2_%d" % t, [P, S], F32)
+            for h, cols in enumerate(halves):
+                if (t, h) not in FUSED:
+                    nc.scalar.activation(other[:, cols], a2[t][:].indirect(entries(n4_l, cols.start, HALF)), COPY)
                 nc.scalar.activation(
-                    ea2[:],
-                    b[t][:].indirect(entries(n3_l, first, width)),
+                    ea2[:, cols],
+                    b[t][:].indirect(entries(n3_l, cols.start, HALF)),
                     EXP,
                     bias=b_bias[t][:],
                     scale=tau2_c[:, t : t + 1],
                 )
-                diff = sb("diff" + tag, [P, width], F32)
-                nc.vector.scalar_tensor_tensor(diff[:], accs[t][0][:, cols], 0.125, other[:], MULT, SUB)
-                prod = sb("prod" + tag, [P, width], F32)
-                (nc.gpsimd if (t, first) in PROD_G else nc.vector).tensor_tensor(prod[:], diff[:], ea2[:], MULT)
-                nc.vector.scalar_tensor_tensor(res[:, t, :], accs[t][1][:, cols], -0.03125, prod[:], MULT, ADD)
-                nc.sync.dma_start(out_rows[:, t, cols], res[:, t, :])
-            res_in = sb("res_in%d" % first, [P, width, PACK], BF16)
-            if first in IL_S:
-                nc.scalar.copy(res_in[:], res[:].rearrange("p t c -> p c t"))
-            else:
-                nc.vector.tensor_copy(res_in[:], res[:].rearrange("p t c -> p c t"))
-            nc.vector.quantize_mx(
-                out=o_w[:, cols].bitcast(FP8X4), scales=o_s[:, cols], in_=res_in[:].rearrange("p c t -> p (c t)")
-            )
-            nc.sync.dma_start(
-                out_1[0].rearrange("p n t -> p (n t)").bitcast(I32)[:, cols], o_w[:, cols].bitcast(I32)
-            )
+            for h, cols in enumerate(halves if t in SPLIT else whole):
+                u = len(units)
+                units.append(u)
+                width = cols.stop - cols.start
+                diff = sb("diff%d" % u, [P, width], F32, "work%d" % ((2 * u) % RING))
+                if (t, h) in FUSED:
+                    nc.vector.tensor_tensor(diff[:], a2[t][:].indirect(entries(n4_l, cols.start, HALF)), twins[t][:, cols], SUB)
+                else:
+                    nc.vector.tensor_tensor(diff[:], other[:, cols], a2[t][:, cols], SUB)
+                prod = sb("prod%d" % u, [P, width], F32, "work%d" % ((2 * u + 1) % RING))
+                (nc.gpsimd if t in PROD_G else nc.vector).tensor_tensor(prod[:], diff[:], ea2[:, cols], MULT)
+                nc.vector.scalar_tensor_tensor(res[:, t, cols], b[t][:, cols], -0.5, prod[:], MULT, SUB)
+                nc.sync.dma_start(out_rows[:, t, cols], res[:, t, cols])
+                if t == PACK - 1:
+                    interleave(h, slice(2, 4))
+                    nc.vector.quantize_mx(
+                        out=o_w[:, cols].bitcast(FP8X4), scales=o_s[:, cols], in_=res_in[h][:].rearrange("p c t -> p (c t)")
+                    )
+                    nc.sync.dma_start(
+                        out_1[0].rearrange("p n t -> p (n t)").bitcast(I32)[:, cols], o_w[:, cols].bitcast(I32)
+                    )
+            if t == 1:
+                for h in range(2):
+                    interleave(h, slice(0, 2))
+
+        for t in range(AHEAD):
+            open_rows(t)
+        for t in range(PACK):
+            if t + AHEAD < PACK:
+                open_rows(t + AHEAD)
+            close_rows(t)
         for q in range(4):
             queue = nc.scalar if q % 2 == 0 else nc.sync
             queue.dma_start(out_2[0, 4 * q : 4 * q + 4, :].bitcast(I32), o_s[32 * q : 32 * q + 4, :].bitcast(I32))

@@ -24,12 +24,13 @@ MAX = mybir.AluOpType.max
 EXP = mybir.ActivationFunctionType.Exp
 COPY = mybir.ActivationFunctionType.Copy
 
-A_ON_VECTOR = (1, 2, 3)
+A_ON_VECTOR = (1,)
 PROD_G = ()
 SPLIT = (0, 1, 2, 3)
 AHEAD = 4
+ZI_S = ()
 IL_S = ((0, 0), (0, 1))
-FUSED = ()
+FUSED = ((1, 0), (1, 1))
 RING = 99
 
 
@@ -171,15 +172,16 @@ def tile_picked_cdhpxbesd_none_po_kernel(
         z_w = sb("z_w", [P, S], U32)
         z_s = sb("z_s", [P, S], U8)
 
-        def make_z(t):
-            halves = []
+        def make_z(pair):
+            rows = [sb("z_pair%d" % h, [P, 2, HALF], BF16) for h in range(2)]
+            for t in (pair, pair + 1):
+                for h, cols in enumerate(halves):
+                    nc.vector.scalar_tensor_tensor(
+                        rows[h][:, t - pair, :], y[t][:, cols], gs_y[:, t : t + 1], ds[t][:, cols], MULT, ADD
+                    )
             for h in range(2):
-                cols = slice(h * HALF, (h + 1) * HALF)
-                z_half = sb("z_half%d" % h, [P, HALF], BF16)
-                nc.vector.scalar_tensor_tensor(z_half[:], y[t][:, cols], gs_y[:, t : t + 1], ds[t][:, cols], MULT, ADD)
-                halves.append(z_half)
-            for h in range(2):
-                nc.vector.tensor_copy(z_in[h][:, :, t], halves[h][:])
+                copy = nc.scalar.copy if (pair, h) in ZI_S else nc.vector.tensor_copy
+                copy(z_in[h][:, :, pair : pair + 2], rows[h][:].rearrange("p t c -> p c t"))
 
         hc_w = sb("hc_w", [P, S], U32)
         hc_s_dealt = sb("hc_s_dealt", [P, S], U8)
@@ -224,8 +226,8 @@ def tile_picked_cdhpxbesd_none_po_kernel(
                     put_sm(t, h)
         for pick in picks:
             pick()
-        for t in range(PACK):
-            make_z(t)
+        for pair in range(0, PACK, 2):
+            make_z(pair)
         ca_w, ca_s = picked["ca_w"], picked["ca_s"]
         for h in range(2):
             cols = slice(h * HALF, (h + 1) * HALF)
@@ -238,6 +240,7 @@ def tile_picked_cdhpxbesd_none_po_kernel(
         o_s = sb("o_s", [P, S], U8)
         res = sb("res", [P, PACK, S], F32)
         res_in = [sb("res_in%d" % h, [P, HALF, PACK], BF16) for h in range(2)]
+        kept = []
         twins, banks, a2, b, b_bias, units = [], [], [], [], [], []
 
         def open_rows(t):
@@ -256,6 +259,7 @@ def tile_picked_cdhpxbesd_none_po_kernel(
             if t in A_ON_VECTOR:
                 nc.vector.tensor_scalar(rows_a[:], accs_a[0][:], 0.125, None, MULT)
             a2.append(rows_a)
+            kept.append((accs_a[0], accs_b[0]))
             twin = None
             if any(tt == t for tt, hh in FUSED):
                 twin = sb("a2_twin%d" % t, [P, S], F32)
@@ -289,11 +293,16 @@ def tile_picked_cdhpxbesd_none_po_kernel(
                 diff = sb("diff%d" % u, [P, width], F32, "work%d" % ((2 * u) % RING))
                 if (t, h) in FUSED:
                     nc.vector.tensor_tensor(diff[:], a2[t][:].indirect(entries(n4_l, cols.start, HALF)), twins[t][:, cols], SUB)
+                elif t in PROD_G:
+                    nc.vector.scalar_tensor_tensor(diff[:], kept[t][0][:, cols], -0.125, other[:, cols], MULT, ADD)
                 else:
                     nc.vector.tensor_tensor(diff[:], other[:, cols], a2[t][:, cols], SUB)
                 prod = sb("prod%d" % u, [P, width], F32, "work%d" % ((2 * u + 1) % RING))
                 (nc.gpsimd if t in PROD_G else nc.vector).tensor_tensor(prod[:], diff[:], ea2[:, cols], MULT)
-                nc.vector.scalar_tensor_tensor(res[:, t, cols], b[t][:, cols], -0.5, prod[:], MULT, SUB)
+                if t in PROD_G:
+                    nc.vector.scalar_tensor_tensor(res[:, t, cols], kept[t][1][:, cols], -0.03125, prod[:], MULT, SUB)
+                else:
+                    nc.vector.scalar_tensor_tensor(res[:, t, cols], b[t][:, cols], -0.5, prod[:], MULT, SUB)
                 nc.sync.dma_start(out_rows[:, t, cols], res[:, t, cols])
                 if t == PACK - 1:
                     interleave(h, slice(2, 4))

@@ -65,21 +65,27 @@ def tile_picked_cdhpxbesd_none_po_kernel(
                 nc.sync.dma_start(plane[32 * q : 32 * q + 32, :].bitcast(I32), rows.partition_broadcast(8))
 
         xs = sb("xs", [P, T], U8)
-        load_plane(xs, x_scales, range(4))
+        nc.gpsimd.memset(xs[:].bitcast(I32), 0)
+        for q in range(4):
+            nc.sync.dma_start(xs[32 * q : 32 * q + 4, :].bitcast(I32), x_scales[0, 4 * q : 4 * q + 4, :].bitcast(I32))
         offs_l = load_list("offs_l", offs)
         w1s_raw = sb("w1s_raw", [P, S], U8)
-        load_plane(w1s_raw, w1_scales, range(2))
-        xw = sb("xw", [P, T], U32)
-        nc.sync.dma_start(xw[:].bitcast(I32), x_words[0].rearrange("p n t -> p (n t)").bitcast(I32))
-        load_plane(w1s_raw, w1_scales, range(2, 4))
         w1w_raw = sb("w1w_raw", [P, 2 * S], U8)
         nc.sync.dma_start(w1w_raw[:].bitcast(I32), w1_words[0].bitcast(I32))
+        load_plane(w1s_raw, w1_scales, range(1))
+        xw = sb("xw", [P, T], U32)
+        nc.sync.dma_start(xw[:].bitcast(I32), x_words[0].rearrange("p n t -> p (n t)").bitcast(I32))
+        load_plane(w1s_raw, w1_scales, range(1, 4))
         tau_c = load_rows("tau_c", tau)
         n1_l = load_list("n1_l", n1)
         gs_c = load_rows("gs_c", gs)
         n2_l = load_list("n2_l", n2)
         ca_l = load_list("ca_l", ca)
         hc_l = load_list("hc_l", hc)
+        xs_runs = sb("xs_runs", [P, T], U8)
+        nc.gpsimd.memset(xs_runs[:].bitcast(I32), 0)
+        for e in range(2):
+            nc.sync.dma_start(xs_runs[e:P:16, :].bitcast(I32), x_scales[0, e:16:2, :].bitcast(I32))
         tau2_c = load_rows("tau2_c", tau2)
         n3_l = load_list("n3_l", n3)
         n4_l = load_list("n4_l", n4)
@@ -191,12 +197,12 @@ def tile_picked_cdhpxbesd_none_po_kernel(
 
         def pick_hc_scales():
             hc_s_raw = sb("hc_s_raw", [P, S], U8, "ea0")
-            nc.vector.tensor_copy(hc_s_raw[:], xs[:].indirect(hc_l[:]))
+            nc.vector.tensor_copy(hc_s_raw[:], xs_runs[:].indirect(hc_l[:]))
             nc.vector.tensor_copy(
                 hc_s_dealt[:].rearrange("p (t m) -> p t m", t=PACK), hc_s_raw[:].rearrange("p (m t) -> p t m", t=PACK)
             )
             for r in range(4):
-                src = r + 16 * (r // 2)
+                src = r % 2 + 16 * (r // 2)
                 nc.sync.dma_start(hc_s[r:P:32, :].bitcast(I32), hc_s_dealt[src:P:32, :].bitcast(I32))
 
         def pick_hc_words():

from contextlib import ExitStack

import concourse.mybir as mybir

K, T, S = 512, 2048, 512
P = 128
PACK = 4
HALF = S // 2
LIST_COLS = S // 16
FLOPS = 3 * 2 * K * S * S

F32 = mybir.dt.float32
BF16 = mybir.dt.bfloat16
I32 = mybir.dt.int32
U32 = mybir.dt.uint32
U16 = mybir.dt.uint16
U8 = mybir.dt.uint8
FP8X4 = mybir.dt.float8_e4m3fn_x4
FP4X4 = mybir.dt.float4_e2m1fn_x4
MULT = mybir.AluOpType.mult
ADD = mybir.AluOpType.add
SUB = mybir.AluOpType.subtract
MAX = mybir.AluOpType.max
EXP = mybir.ActivationFunctionType.Exp
COPY = mybir.ActivationFunctionType.Copy

A_ON_VECTOR = (1,)
PROD_G = ()
SPLIT = (0, 1, 2, 3)
AHEAD = 4
ZI_S = ()
IL_S = ((0, 0), (0, 1))
FUSED = ((1, 0), (1, 1))
RING = 99


def entries(lst, first, count):
    return lst[:, first // 16 : (first + count) // 16]


def tile_picked_cdhpxbesd_none_po_kernel(
    tc, x_words, x_scales, w1_words, w1_scales, tau, gs, tau2, offs, n1, n2, ca, hc, n3, n4, out_0, out_1, out_2
):
    nc = tc.nc
    with ExitStack() as ctx:
        keep = ctx.enter_context(tc.tile_pool(name="keep", bufs=1))
        psum = ctx.enter_context(tc.psum_pool(name="psum", bufs=1))

        def sb(name, shape, dtype, tag=None):
            return keep.tile(shape, dtype, name=name, tag=tag or name, align_bytes=64)

        def load_list(name, src):
            lst = sb(name, [P, LIST_COLS], U16)
            nc.sync.dma_start(lst[:], src)
            return lst

        def load_rows(name, src):
            col = sb(name, [P, PACK], F32)
            nc.sync.dma_start(col[:], src.rearrange("(p t) o -> p (t o)", t=PACK))
            return col

        def load_plane(plane, src, quadrants):
            for q in quadrants:
                rows = src[0, 4 * q : 4 * q + 4, :].bitcast(I32)
                nc.sync.dma_start(plane[32 * q : 32 * q + 32, :].bitcast(I32), rows.partition_broadcast(8))

        xs = sb("xs", [P, T], U8)
        nc.gpsimd.memset(xs[:].bitcast(I32), 0)
        for q in range(4):
            nc.sync.dma_start(xs[32 * q : 32 * q + 4, :].bitcast(I32), x_scales[0, 4 * q : 4 * q + 4, :].bitcast(I32))
        offs_l = load_list("offs_l", offs)
        w1s_raw = sb("w1s_raw", [P, S], U8)
        w1w_raw = sb("w1w_raw", [P, 2 * S], U8)
        nc.sync.dma_start(w1w_raw[:].bitcast(I32), w1_words[0].bitcast(I32))
        load_plane(w1s_raw, w1_scales, range(1))
        xw = sb("xw", [P, T], U32)
        nc.sync.dma_start(xw[:].bitcast(I32), x_words[0].rearrange("p n t -> p (n t)").bitcast(I32))
        load_plane(w1s_raw, w1_scales, range(1, 4))
        tau_c = load_rows("tau_c", tau)
        n1_l = load_list("n1_l", n1)
        gs_c = load_rows("gs_c", gs)
        n2_l = load_list("n2_l", n2)
        ca_l = load_list("ca_l", ca)
        hc_l = load_list("hc_l", hc)
        xs_runs = sb("xs_runs", [P, T], U8)
        nc.gpsimd.memset(xs_runs[:].bitcast(I32), 0)
        for e in range(2):
            nc.sync.dma_start(xs_runs[e:P:16, :].bitcast(I32), x_scales[0, e:16:2, :].bitcast(I32))
        tau2_c = load_rows("tau2_c", tau2)
        n3_l = load_list("n3_l", n3)
        n4_l = load_list("n4_l", n4)

        xq_s = sb("xq_s", [P, S], U8)
        nc.vector.tensor_copy(xq_s[:], xs[:].indirect(offs_l[:]))
        w1w = sb("w1w", [P, PACK, P], U16)
        w1w_dealt = w1w_raw[:].bitcast(U16).rearrange("p (m t) -> p t m", t=PACK)
        w1s = sb("w1s", [P, PACK, P], U8)
        w1s_dealt = w1s_raw[:].rearrange("p (m t) -> p t m", t=PACK)
        xq_w = sb("xq_w", [P, S], U32)
        for h, planes in enumerate((slice(0, 1), slice(1, PACK))):
            nc.scalar.copy(w1w[:, planes, :], w1w_dealt[:, planes, :])
            nc.vector.tensor_copy(xq_w[:, h * HALF : (h + 1) * HALF], xw[:].indirect(entries(offs_l, h * HALF, HALF)))
            nc.gpsimd.tensor_copy(w1s[:, planes, :], w1s_dealt[:, planes, :])
        neg_tau = sb("neg_tau", [P, PACK], F32)
        nc.vector.tensor_scalar(neg_tau[:], tau_c[:], -1.0, None, MULT)
        neg_tau2 = sb("neg_tau2", [P, PACK], F32)
        nc.gpsimd.tensor_scalar(neg_tau2[:], tau2_c[:], -1.0, 0.0, MULT, ADD)
        gs_sm = sb("gs_sm", [P, PACK], F32)
        nc.gpsimd.tensor_scalar(gs_sm[:], gs_c[:], 2.0, 0.0, MULT, ADD)
        gs_y = sb("gs_y", [P, PACK], F32)
        nc.gpsimd.tensor_scalar(gs_y[:], gs_c[:], -0.5, 0.0, MULT, ADD)

        def product(bank, lhs_w, lhs_s, rhs_w, rhs_s, cols):
            acc = psum.tile([P, cols.stop - cols.start], F32, name="bank%d" % bank)
            nc.tensor.matmul_mx(
                out=acc[:],
                lhsT=lhs_w,
                lhsT_scale=lhs_s,
                rhs=rhs_w[:, cols].bitcast(FP8X4),
                rhs_scale=rhs_s[:, cols],
                start=True,
                stop=True,
            )
            return acc

        def leave_banks_with_bias(name, accs, factor, rate, on_scalar=False):
            rows = sb(name, [P, S], F32)
            width = S // len(accs)
            top = None
            for i, acc in enumerate(accs):
                so_far = top
                top = sb("%s_top%d" % (name, i), [P, 1], F32)[:]
                nc.vector.tensor_scalar(
                    rows[:, i * width : (i + 1) * width], acc[:], factor, so_far, MULT, MAX, accum_out=top
                )
            bias = sb(name + "_bias", [P, 1], F32)
            if on_scalar:
                nc.scalar.activation(bias[:], top, COPY, scale=rate)
            else:
                nc.gpsimd.tensor_scalar(bias[:], top, rate, 0.0, MULT, ADD)
            return rows, bias

        halves = [slice(0, HALF), slice(HALF, S)]
        whole = [slice(0, S)]
        y, y_bias = [], []
        for t in range(PACK):
            accs = [
                product(t + 4 * i, w1w[:, t, :].bitcast(FP4X4), w1s[:, t, :], xq_w, xq_s, cols)
                for i, cols in enumerate(halves if t == 0 else whole)
            ]
            rows, bias = leave_banks_with_bias("y%d" % t, accs, 1.0, neg_tau[:, t : t + 1], t == 0)
            y.append(rows)
            y_bias.append(bias)

        sm = [sb("sm%d" % t, [P, S], F32) for t in range(PACK)]
        ds = [sb("ds%d" % t, [P, S], F32) for t in range(PACK)]
        ea = [sb("ea%d" % t, [P, S], F32) for t in range(PACK)]

        def fetch_ea(t, h):
            cols = slice(h * HALF, (h + 1) * HALF)
            nc.scalar.activation(
                ea[t][:, cols],
                y[t][:].indirect(entries(n1_l, h * HALF, HALF)),
                EXP,
                bias=y_bias[t][:],
                scale=tau_c[:, t : t + 1],
            )

        def make_sm(t, h):
            cols = slice(h * HALF, (h + 1) * HALF)
            nc.vector.scalar_tensor_tensor(sm[t][:, cols], y[t][:, cols], gs_sm[:, t : t + 1], ea[t][:, cols], MULT, MULT)

        def put_sm(t, h):
            cols = slice(h * HALF, (h + 1) * HALF)
            nc.scalar.activation(ds[t][:].indirect(entries(n2_l, h * HALF, HALF)), sm[t][:, cols], COPY)

        z_in = [sb("z_in%d" % h, [P, HALF, PACK], BF16) for h in range(2)]
        z_w = sb("z_w", [P, S], U32)
        z_s = sb("z_s", [P, S], U8)

        def make_z(pair):
            rows = [sb("z_pair%d" % h, [P, 2, HALF], BF16) for h in range(2)]
            for t in (pair, pair + 1):
                for h, cols in enumerate(halves):
                    nc.vector.scalar_tensor_tensor(
                        rows[h][:, t - pair, :], y[t][:, cols], gs_y[:, t : t + 1], ds[t][:, cols], MULT, ADD
                    )
            for h in range(2):
                copy = nc.scalar.copy if (pair, h) in ZI_S else nc.vector.tensor_copy
                copy(z_in[h][:, :, pair : pair + 2], rows[h][:].rearrange("p t c -> p c t"))

        hc_w = sb("hc_w", [P, S], U32)
        hc_s_dealt = sb("hc_s_dealt", [P, S], U8)
        hc_s = sb("hc_s", [P, S], U8)
        nc.gpsimd.memset(hc_s[:].bitcast(I32), 0)
        picked = {}

        def pick_hc_scales():
            hc_s_raw = sb("hc_s_raw", [P, S], U8, "ea0")
            nc.vector.tensor_copy(hc_s_raw[:], xs_runs[:].indirect(hc_l[:]))
            nc.vector.tensor_copy(
                hc_s_dealt[:].rearrange("p (t m) -> p t m", t=PACK), hc_s_raw[:].rearrange("p (m t) -> p t m", t=PACK)
            )
            for r in range(4):
                src = r % 2 + 16 * (r // 2)
                nc.sync.dma_start(hc_s[r:P:32, :].bitcast(I32), hc_s_dealt[src:P:32, :].bitcast(I32))

        def pick_hc_words():
            hc_w_raw = sb("hc_w_raw", [P, S], U32, "ea1")
            nc.vector.tensor_copy(hc_w_raw[:], xw[:].indirect(hc_l[:]))
            nc.vector.tensor_copy(
                hc_w[:].rearrange("p (t m) -> p t m", t=PACK), hc_w_raw[:].rearrange("p (m t) -> p t m", t=PACK)
            )

        def pick_ca_words():
            picked["ca_w"] = sb("ca_w", [P, S], U32, "ea2")
            nc.vector.tensor_copy(picked["ca_w"][:].rearrange("p (t m) -> p m t", t=PACK), xw[:].indirect(ca_l[:]))

        def pick_ca_scales():
            picked["ca_s"] = sb("ca_s", [P, S], U8, "ea3")
            nc.vector.tensor_copy(picked["ca_s"][:].rearrange("p (t m) -> p m t", t=PACK), xs[:].indirect(ca_l[:]))

        picks = [pick_hc_scales, pick_hc_words, pick_ca_words, pick_ca_scales]

        for t in range(PACK):
            for h in range(2):
                fetch_ea(t, h)
        for pair in range(0, PACK, 2):
            for h in range(2):
                for t in (pair, pair + 1):
                    make_sm(t, h)
                    put_sm(t, h)
        for pick in picks:
            pick()
        for pair in range(0, PACK, 2):
            make_z(pair)
        ca_w, ca_s = picked["ca_w"], picked["ca_s"]
        for h in range(2):
            cols = slice(h * HALF, (h + 1) * HALF)
            nc.vector.quantize_mx(
                out=z_w[:, cols].bitcast(FP8X4), scales=z_s[:, cols], in_=z_in[h][:].rearrange("p c t -> p (c t)")
            )

        out_rows = out_0.rearrange("(p t) j -> p t j", t=PACK)
        o_w = sb("o_w", [P, S], U32)
        o_s = sb("o_s", [P, S], U8)
        res = sb("res", [P, PACK, S], F32)
        res_in = [sb("res_in%d" % h, [P, HALF, PACK], BF16) for h in range(2)]
        kept = []
        twins, banks, a2, b, b_bias, units = [], [], [], [], [], []

        def open_rows(t):
            m_cols = slice(P * t, P * (t + 1))
            accs_a, accs_b = [], []
            for cols in halves if t == 0 else whole:
                for accs_x, words, scales in ((accs_a, ca_w, ca_s), (accs_b, hc_w, hc_s)):
                    bank = (5 + len(banks)) % 8
                    banks.append(bank)
                    accs_x.append(product(bank, words[:, m_cols].bitcast(FP8X4), scales[:, m_cols], z_w, z_s, cols))
            rows_a = sb("a2_%d" % t, [P, S], F32)
            if t not in A_ON_VECTOR:
                for acc, cols in zip(accs_a, halves if t == 0 else whole):
                    nc.scalar.activation(rows_a[:, cols], acc[:], COPY, scale=0.125)
            rows, bias = leave_banks_with_bias("b%d" % t, accs_b, 0.0625, neg_tau2[:, t : t + 1])
            if t in A_ON_VECTOR:
                nc.vector.tensor_scalar(rows_a[:], accs_a[0][:], 0.125, None, MULT)
            a2.append(rows_a)
            kept.append((accs_a[0], accs_b[0]))
            twin = None
            if any(tt == t for tt, hh in FUSED):
                twin = sb("a2_twin%d" % t, [P, S], F32)
                nc.sync.dma_start(twin[:], rows_a[:])
            twins.append(twin)
            b.append(rows)
            b_bias.append(bias)

        def interleave(h, planes):
            copy = nc.scalar.copy if (planes.start, h) in IL_S else nc.vector.tensor_copy
            copy(res_in[h][:, :, planes], res[:, planes, halves[h]].rearrange("p t c -> p c t"))

        def close_rows(t):
            if (t, 0) not in FUSED or (t, 1) not in FUSED:
                other = sb("other%d" % t, [P, S], F32)
            ea2 = sb("ea2_%d" % t, [P, S], F32)
            for h, cols in enumerate(halves):
                if (t, h) not in FUSED:
                    nc.scalar.activation(other[:, cols], a2[t][:].indirect(entries(n4_l, cols.start, HALF)), COPY)
                nc.scalar.activation(
                    ea2[:, cols],
                    b[t][:].indirect(entries(n3_l, cols.start, HALF)),
                    EXP,
                    bias=b_bias[t][:],
                    scale=tau2_c[:, t : t + 1],
                )
            for h, cols in enumerate(halves if t in SPLIT else whole):
                u = len(units)
                units.append(u)
                width = cols.stop - cols.start
                diff = sb("diff%d" % u, [P, width], F32, "work%d" % ((2 * u) % RING))
                if (t, h) in FUSED:
                    nc.vector.tensor_tensor(diff[:], a2[t][:].indirect(entries(n4_l, cols.start, HALF)), twins[t][:, cols], SUB)
                elif t in PROD_G:
                    nc.vector.scalar_tensor_tensor(diff[:], kept[t][0][:, cols], -0.125, other[:, cols], MULT, ADD)
                else:
                    nc.vector.tensor_tensor(diff[:], other[:, cols], a2[t][:, cols], SUB)
                prod = sb("prod%d" % u, [P, width], F32, "work%d" % ((2 * u + 1) % RING))
                (nc.gpsimd if t in PROD_G else nc.vector).tensor_tensor(prod[:], diff[:], ea2[:, cols], MULT)
                if t in PROD_G:
                    nc.vector.scalar_tensor_tensor(res[:, t, cols], kept[t][1][:, cols], -0.03125, prod[:], MULT, SUB)
                else:
                    nc.vector.scalar_tensor_tensor(res[:, t, cols], b[t][:, cols], -0.5, prod[:], MULT, SUB)
                nc.sync.dma_start(out_rows[:, t, cols], res[:, t, cols])
                if t == PACK - 1:
                    interleave(h, slice(2, 4))
                    nc.vector.quantize_mx(
                        out=o_w[:, cols].bitcast(FP8X4), scales=o_s[:, cols], in_=res_in[h][:].rearrange("p c t -> p (c t)")
                    )
                    nc.sync.dma_start(
                        out_1[0].rearrange("p n t -> p (n t)").bitcast(I32)[:, cols], o_w[:, cols].bitcast(I32)
                    )
            if t == 1:
                for h in range(2):
                    interleave(h, slice(0, 2))

        for t in range(AHEAD):
            open_rows(t)
        for t in range(PACK):
            if t + AHEAD < PACK:
                open_rows(t + AHEAD)
            close_rows(t)
        for q in range(4):
            queue = nc.scalar if q % 2 == 0 else nc.sync
            queue.dma_start(out_2[0, 4 * q : 4 * q + 4, :].bitcast(I32), o_s[32 * q : 32 * q + 4, :].bitcast(I32))
